import numpy as np
import ml_dtypes


def mxq(x, axis, fmt="e4m3"):
    dtype, down = {"e4m3": (ml_dtypes.float8_e4m3fn, 7), "e5m2": (ml_dtypes.float8_e5m2, 14)}[fmt]
    v = np.moveaxis(np.asarray(x, np.float32).astype(ml_dtypes.bfloat16).astype(np.float64), axis, -1)
    blocks = v.reshape(v.shape[:-1] + (-1, 32))
    amax = np.abs(blocks).max(-1, keepdims=True)
    byte = np.maximum(np.where(amax > 0, np.frexp(amax)[1] - 1 + 127, 0) - down, 1)
    scale = np.exp2(byte - 127.0)
    codes = (blocks / scale).astype(np.float32).astype(dtype).astype(np.float64)
    return np.moveaxis((codes * scale).reshape(v.shape), -1, axis)


WIDE = False


def mx_kscale(k):
    if not WIDE:
        return np.ones(k)
    levels = np.array([10, -10, 5, -5, 0])
    if k % 512:
        return np.exp2(np.random.permutation(np.resize(levels, k // 32))).repeat(32)
    a = np.empty((k // 512, 16))
    for p in range(k // 512):
        a[p, :8] = np.random.permutation(np.resize(levels, 8))
        for g in range(8):
            far = levels[np.abs(levels - a[p, g]) >= 10]
            a[p, g + 8] = far[np.random.randint(len(far))]
    return np.exp2(a.ravel()).repeat(32)


def f64(x):
    return np.asarray(x).astype(np.float64)


def striped(idx):
    return np.tile(idx.reshape(-1, 16).T, (8, 1)).astype(np.uint16)


def unstriped(offs):
    return offs[:16].T.reshape(-1).astype(np.int64)


def pack_weight(w):
    k, n = w.shape
    w = f64(np.asarray(w, np.float32).astype(ml_dtypes.bfloat16)).reshape(k // 32, 32, n)
    amax = np.abs(w).max(1)
    byte = np.clip(np.where(amax > 0, np.frexp(amax)[1] - 1 + 127 - 7, 1), 1, 254)
    scaled = (w * np.exp2(127.0 - byte)[:, None, :]).reshape(k, n).astype(np.float32)
    words = np.ascontiguousarray(scaled.reshape(k // 512, 128, 4, n).transpose(0, 1, 3, 2)).astype(ml_dtypes.float8_e4m3fn).view(np.uint8)
    return words, np.ascontiguousarray(byte.astype(np.uint8).reshape(k // 512, 16, n))


def unpack_weight(words, scales):
    g, p, n, _ = words.shape
    vals = np.ascontiguousarray(words).view(ml_dtypes.float8_e4m3fn).astype(np.float64) * np.repeat(np.exp2(scales.astype(np.float64) - 127.0), 8, axis=1)[..., None]
    return vals.transpose(0, 1, 3, 2).reshape(g * 512, n)


K, T, S, D, N, H = 1024, 2048, 1024, 2, 128, 512


def setup_inputs():
    n = np.random.standard_normal
    s = mx_kscale(K)[:, None]
    u = mx_kscale(H)
    packed_xT = pack_weight(n((K, T)) * s)
    return {
        "x_words": packed_xT[0],
        "x_scales": packed_xT[1],
        "w1": (n((K, H)) / np.sqrt(K) / s).astype(np.float32),
        "w2": (n((K, H)) / np.sqrt(K) / s).astype(np.float32),
        "unit": (np.random.uniform(0.6, 1.4, (H, 1)) * u[:, None]).astype(np.float32),
        "w3": (n((H, N)) / np.sqrt(H) / u[:, None]).astype(np.float32),
        "offs": striped(np.random.permutation(T)[:S]),
        "ovl": striped(np.random.permutation(S)),
    }


def reference(x_words, x_scales, w1, w2, unit, w3, offs, ovl):
    xq = unpack_weight(x_words, x_scales)[:, unstriped(offs)]
    mt = mxq(f64(w1), 0, "e4m3").T @ xq
    tmem = np.log(np.exp(mt) + 1.0)
    ft = mxq(f64(w2), 0, "e4m3").T @ xq
    tflop = np.log(np.exp(ft) + 1.0)
    roof = np.maximum(tmem, tflop)
    tmo = tmem[:, unstriped(ovl)]
    hidd = np.minimum(tmo, tflop)
    exec_ = roof + 0.3 * (tmem + tflop - roof) - (0.6 * hidd)
    wave = exec_.reshape(len(exec_), -1, D).max(axis=2)
    imb = np.repeat(wave, D, axis=1) - exec_
    hid = f64(unit) * (exec_ - (0.5 * imb))
    return mxq(f64(w3), 0, "e4m3").T @ mxq(hid, 0, "e4m3")

@@ -1,0 +1,292 @@
+from contextlib import ExitStack
+
+import concourse.mybir as mybir
+
+K, T, S, H, N = 1024, 2048, 1024, 512, 128
+FLOPS = 2 * (2 * K * H * S + H * N * S)
+
+F32 = mybir.dt.float32
+BF16 = mybir.dt.bfloat16
+I32 = mybir.dt.int32
+U32 = mybir.dt.uint32
+U16 = mybir.dt.uint16
+U8 = mybir.dt.uint8
+FP8X4 = mybir.dt.float8_e4m3fn_x4
+ALU = mybir.AluOpType
+ACT = mybir.ActivationFunctionType
+
+P = 128
+PACK = 4
+PASSES = K // (P * PACK)
+BANK = 512
+HALVES = S // BANK
+LN_FLOOR = 2.0**-60
+
+
+def tile_picked_ygpusch_bal_p_kernel(
+    tc, x_words, x_scales, w1, w2, unit, w3, offs, ovl, out
+):
+    nc = tc.nc
+    with ExitStack() as ctx:
+        keep = ctx.enter_context(tc.tile_pool(name="keep", bufs=1))
+        work = ctx.enter_context(tc.tile_pool(name="work", bufs=2))
+        psum = ctx.enter_context(tc.psum_pool(name="psum", bufs=8))
+
+        offs_t = keep.tile([P, S // 16], U16, name="offs_t")
+        ovl_t = keep.tile([P, S // 16], U16, name="ovl_t")
+        x_win = [keep.tile([P, T], I32, name=f"x_win{o}", align_bytes=64) for o in range(PASSES)]
+        xs_win = keep.tile([P, T], U8, name="xs_win", align_bytes=64)
+        x_codes = [keep.tile([P, S], U32, name=f"x_codes{o}", align_bytes=64) for o in range(PASSES)]
+        x_bytes = keep.tile([P, S], U8, name="x_bytes", align_bytes=64)
+        weights = (w1, w2)
+        w_raw, w_bf, w_codes, w_bytes = {}, {}, {}, {}
+        for o in range(PASSES):
+            for i in range(2):
+                pieces = 2 if (i, o) == (1, PASSES - 1) else 1
+                w_raw[i, o] = [
+                    keep.tile([P, PACK, H // pieces], F32, name=f"w_raw{i}{o}{n}") for n in range(pieces)
+                ]
+                w_bf[i, o] = keep.tile([P, PACK * H], BF16, name=f"w_bf{i}{o}", align_bytes=64)
+                w_codes[i, o] = keep.tile([P, H], U32, name=f"w_codes{i}{o}", align_bytes=64)
+                w_bytes[i, o] = keep.tile([P, H], U8, name=f"w_bytes{i}{o}", align_bytes=64)
+        w3_raw = keep.tile([P, PACK, N], F32, name="w3_raw")
+        w3_bf = keep.tile([P, PACK * N], BF16, name="w3_bf", align_bytes=64)
+        w3_codes = keep.tile([P, N], U32, name="w3_codes", align_bytes=64)
+        w3_bytes = keep.tile([P, N], U8, name="w3_bytes", align_bytes=64)
+        unit_t = keep.tile([P, PACK], F32, name="unit_t")
+        own_gain = keep.tile([P, PACK], F32, name="own_gain")
+        wave_gain = keep.tile([P, PACK], F32, name="wave_gain")
+        ln_floor = keep.tile([P, 1], F32, name="ln_floor")
+        hid = keep.tile([P, PACK, S], BF16, name="hid")
+
+        nc.vector.memset(xs_win[:].bitcast(I32), 0)
+        nc.vector.memset(ln_floor[:], LN_FLOOR)
+
+        def load_words(o):
+            nc.sync.dma_start(out=x_win[o][:], in_=x_words[o].rearrange("p n t -> p (n t)").bitcast(I32))
+
+        def load_weight(i, o):
+            rows = weights[i][o * P * PACK : (o + 1) * P * PACK, :].rearrange("(p j) c -> p j c", j=PACK)
+            width = H // len(w_raw[i, o])
+            for n, piece in enumerate(w_raw[i, o]):
+                nc.sync.dma_start(out=piece[:], in_=rows[:, :, n * width : (n + 1) * width])
+
+        nc.sync.dma_start(offs_t[:], offs)
+        load_words(0)
+        for q in range(4):
+            nc.sync.dma_start(
+                out=xs_win[32 * q : 32 * q + 4 * PASSES, :].bitcast(I32),
+                in_=x_scales[:, 4 * q : 4 * q + 4, :].bitcast(I32),
+            )
+        load_weight(0, 0)
+        load_words(1)
+        load_weight(1, 0)
+        load_weight(0, 1)
+        load_weight(1, 1)
+        nc.sync.dma_start(ovl_t[:], ovl)
+        nc.sync.dma_start(out=unit_t[:], in_=unit.rearrange("(p t) o -> p (t o)", t=PACK))
+        nc.sync.dma_start(out=w3_raw[:], in_=w3.rearrange("(p j) n -> p j n", j=PACK))
+
+        def gather_words(o):
+            nc.vector.tensor_copy(x_codes[o][:], x_win[o][:].bitcast(U32).indirect(offs_t[:]))
+
+        def round_weight(i, o, on_scalar):
+            whole_dst = w_bf[i, o][:].rearrange("p (t m j) -> p m j t", t=PACK, j=PACK)
+            width = P // len(w_raw[i, o])
+            for n, piece in enumerate(w_raw[i, o]):
+                dst = whole_dst[:, n * width : (n + 1) * width]
+                src = piece[:].rearrange("p j (m t) -> p m j t", t=PACK)
+                if on_scalar:
+                    nc.scalar.activation(dst, src, ACT.Copy)
+                else:
+                    nc.vector.tensor_copy(dst, src)
+
+        def quantize_weight(i, o, t0, t1):
+            cols = slice(t0 * P, t1 * P)
+            nc.vector.quantize_mx(
+                out=w_codes[i, o][:, cols].bitcast(FP8X4),
+                scales=w_bytes[i, o][:, cols],
+                in_=w_bf[i, o][:, t0 * P * PACK : t1 * P * PACK],
+            )
+
+        gather_words(0)
+        round_weight(0, 0, True)
+        nc.vector.tensor_copy(x_bytes[:], xs_win[:].indirect(offs_t[:]))
+        gather_words(1)
+        round_weight(1, 0, True)
+        quantize_weight(0, 0, 0, 4)
+        quantize_weight(1, 0, 0, 4)
+
+        banks = {}
+
+        def product_pass(i, t, h, o):
+            if o == 0:
+                banks[i, t, h] = psum.tile([P, BANK], F32, name=f"bank{i}{t}{h}", tag="bank")
+            m_cols = slice(t * P, (t + 1) * P)
+            n_cols = slice(h * BANK, (h + 1) * BANK)
+            nc.tensor.matmul_mx(
+                out=banks[i, t, h][:],
+                lhsT=w_codes[i, o][:, m_cols].bitcast(FP8X4),
+                lhsT_scale=w_bytes[i, o][:, m_cols],
+                rhs=x_codes[o][:, n_cols].bitcast(FP8X4),
+                rhs_scale=x_bytes[4 * o : P, n_cols],
+                start=(o == 0),
+                stop=(o == PASSES - 1),
+            )
+
+        sig, neg, soft, picked = {}, {}, {}, {}
+
+        def sigmoids(ts):
+            for t in ts:
+                sig[t] = work.tile([P, 2, S], F32, name=f"sig{t}", tag="sig")
+            for i in range(2):
+                for t in ts:
+                    for h in range(HALVES):
+                        nc.scalar.activation(
+                            sig[t][:, i, h * BANK : (h + 1) * BANK], banks[i, t, h][:], ACT.Sigmoid, scale=-1.0
+                        )
+
+        def logs(ts):
+            for t in ts:
+                neg[t] = work.tile([P, 2, S], F32, name=f"neg{t}", tag="neg")
+                for h in range(HALVES):
+                    cols = slice(h * BANK, (h + 1) * BANK)
+                    nc.scalar.activation(neg[t][:, :, cols], sig[t][:, :, cols], ACT.Ln, bias=ln_floor[:])
+
+        def softplus(i, t, h):
+            if h == 0:
+                soft[i, t] = keep.tile([P, S], F32, name=f"soft{i}{t}")
+            cols = slice(h * BANK, (h + 1) * BANK)
+            nc.vector.scalar_tensor_tensor(
+                soft[i, t][:, cols], neg[t][:, i, cols], -1.0, banks[i, t, h][:], ALU.mult, ALU.max
+            )
+
+        def look_up(t):
+            picked[t] = work.tile([P, S], F32, name=f"picked{t}", tag="picked")
+            for h in range(HALVES):
+                nc.scalar.activation(
+                    picked[t][:, h * BANK : (h + 1) * BANK],
+                    soft[0, t][:].indirect(ovl_t[:, h * BANK // 16 : (h + 1) * BANK // 16]),
+                    ACT.Copy,
+                )
+
+        def steps(t, cols, spare_scalar):
+            a, b = soft[0, t][:, cols], soft[1, t][:, cols]
+            n = cols.stop - cols.start
+            roof = work.tile([P, n], F32, name=f"roof{t}", tag="roof")
+            part = work.tile([P, n], F32, name=f"part{t}", tag="part")
+            both = work.tile([P, n], F32, name=f"both{t}", tag="both")
+            hidd = work.tile([P, n], F32, name=f"hidd{t}", tag="hidd")
+            ex = work.tile([P, n], F32, name=f"ex{t}", tag="ex")
+            wave = work.tile([P, n // 2], F32, name=f"wave{t}", tag="wave")
+            wave_s = work.tile([P, n // 2], F32, name=f"wave_s{t}", tag="wave_s")
+            pairs = ex[:].rearrange("p (v d) -> p v d", d=2)
+
+            def scale_wave():
+                if spare_scalar:
+                    nc.scalar.activation(wave_s[:], wave[:], ACT.Copy, scale=wave_gain[:, t : t + 1])
+                else:
+                    nc.vector.tensor_scalar_mul(wave_s[:], wave[:], wave_gain[:, t : t + 1])
+
+            def make_hid(lo, hi):
+                nc.vector.scalar_tensor_tensor(
+                    hid[:, t, cols.start + lo : cols.start + hi].rearrange("p (v d) -> p v d", d=2),
+                    pairs[:, lo // 2 : hi // 2],
+                    own_gain[:, t : t + 1],
+                    wave_s[:, lo // 2 : hi // 2].unsqueeze(2).to_broadcast([P, (hi - lo) // 2, 2]),
+                    ALU.mult,
+                    ALU.subtract,
+                )
+
+            return make_hid, [
+                lambda: nc.vector.tensor_tensor(roof[:], a, b, ALU.max),
+                lambda: nc.vector.scalar_tensor_tensor(part[:], roof[:], 0.7 / 0.3, a, ALU.mult, ALU.add),
+                lambda: nc.vector.tensor_tensor(both[:], part[:], b, ALU.add),
+                lambda: nc.vector.tensor_tensor(hidd[:], picked[t][:, cols], b, ALU.min),
+                lambda: nc.vector.scalar_tensor_tensor(ex[:], hidd[:], -2.0, both[:], ALU.mult, ALU.add),
+                lambda: nc.vector.tensor_tensor(wave[:], pairs[:, :, 0], pairs[:, :, 1], ALU.max),
+                scale_wave,
+            ]
+
+        def finish(c, OUT_CHUNK, on_scalar):
+            cols = slice(c, c + OUT_CHUNK)
+            grouped = work.tile([P, PACK * OUT_CHUNK], BF16, name=f"grouped{c}", tag="grouped", align_bytes=64)
+            h_codes = work.tile([P, OUT_CHUNK], U32, name=f"h_codes{c}", tag="h_codes", align_bytes=64)
+            h_bytes = work.tile([P, OUT_CHUNK], U8, name=f"h_bytes{c}", tag="h_bytes", align_bytes=64)
+            dst = grouped[:].rearrange("p (c i t) -> p c t i", i=4, t=PACK)
+            src = hid[:, :, cols].rearrange("p t (c i) -> p c t i", i=4)
+            if on_scalar:
+                nc.scalar.copy(dst, src)
+            else:
+                nc.vector.tensor_copy(dst, src)
+            nc.vector.quantize_mx(out=h_codes[:].bitcast(FP8X4), scales=h_bytes[:], in_=grouped[:])
+            acc = psum.tile([P, BANK], F32, name=f"acc{c}", tag="bank")
+            nc.tensor.matmul_mx(
+                out=acc[:, :OUT_CHUNK],
+                lhsT=w3_codes[:].bitcast(FP8X4),
+                lhsT_scale=w3_bytes[:],
+                rhs=h_codes[:].bitcast(FP8X4),
+                rhs_scale=h_bytes[:],
+                start=True,
+                stop=True,
+            )
+            res = work.tile([P, OUT_CHUNK], F32, name=f"res{c}", tag="res")
+            nc.scalar.copy(res[:], acc[:, :OUT_CHUNK])
+            nc.sync.dma_start(out=out[:, cols], in_=res[:])
+
+        first, second = (0, 1), (2, 3)
+        for i in range(2):
+            for t in first:
+                for h in range(HALVES):
+                    product_pass(i, t, h, 0)
+        for i in range(2):
+            round_weight(i, 1, False)
+            quantize_weight(i, 1, 0, 2)
+            for t in first:
+                for h in range(HALVES):
+                    product_pass(i, t, h, 1)
+        sigmoids(first)
+        for i in range(2):
+            quantize_weight(i, 1, 2, 4)
+        nc.vector.tensor_copy(
+            w3_bf[:].rearrange("p (c i j) -> p c j i", i=4, j=PACK),
+            w3_raw[:].rearrange("p j (c i) -> p c j i", i=4),
+        )
+        nc.vector.tensor_scalar_mul(own_gain[:], unit_t[:], 1.5 * 0.3)
+        nc.vector.tensor_scalar_mul(wave_gain[:], unit_t[:], 0.5 * 0.3)
+        nc.vector.quantize_mx(out=w3_codes[:].bitcast(FP8X4), scales=w3_bytes[:], in_=w3_bf[:])
+
+        def softplus_all(ts):
+            logs(ts)
+            for t in ts:
+                for h in range(HALVES):
+                    for i in range(2):
+                        softplus(i, t, h)
+            for t in ts:
+                look_up(t)
+
+        softplus_all(first)
+        for i in range(2):
+            for t in second:
+                for h in range(HALVES):
+                    for o in range(PASSES):
+                        product_pass(i, t, h, o)
+        sigmoids(second)
+        (hid0, steps0), (hid1, steps1) = steps(0, slice(0, S), False), steps(1, slice(0, S), False)
+        for one, other in zip(steps0, steps1):
+            one()
+            other()
+        hid0(0, S)
+        hid1(0, S)
+        softplus_all(second)
+        for h in range(HALVES):
+            cols = slice(h * BANK, (h + 1) * BANK)
+            (hid2, steps2), (hid3, steps3) = steps(2, cols, True), steps(3, cols, True)
+            for one, other in zip(steps2, steps3):
+                one()
+                other()
+            width = BANK if h < HALVES - 1 else BANK // 2
+            for lo in range(0, BANK, width):
+                hid2(lo, lo + width)
+                hid3(lo, lo + width)
+                finish(cols.start + lo, width, cols.start + lo + width < S)

@@ -1,6 +1,7 @@
 from contextlib import ExitStack
 
 import concourse.mybir as mybir
+from concourse.masks import make_identity
 
 K, T, S, H, N = 1024, 2048, 1024, 512, 128
 FLOPS = 2 * (2 * K * H * S + H * N * S)
@@ -20,7 +21,7 @@ PACK = 4
 PASSES = K // (P * PACK)
 BANK = 512
 HALVES = S // BANK
-LN_FLOOR = 2.0**-60
+FLOOR_AT = -40.0
 
 
 def tile_picked_ygpusch_bal_p_kernel(
@@ -44,23 +45,28 @@ def tile_picked_ygpusch_bal_p_kernel(
             for i in range(2):
                 pieces = 2 if (i, o) == (1, PASSES - 1) else 1
                 w_raw[i, o] = [
-                    keep.tile([P, PACK, H // pieces], F32, name=f"w_raw{i}{o}{n}") for n in range(pieces)
+                    keep.tile([P, PACK, H // pieces], F32, name=f"w_raw{i}{o}{n}", tag=f"w_raw{i}{o}{n}", align_bytes=64)
+                    for n in range(pieces)
                 ]
                 w_bf[i, o] = keep.tile([P, PACK * H], BF16, name=f"w_bf{i}{o}", align_bytes=64)
-                w_codes[i, o] = keep.tile([P, H], U32, name=f"w_codes{i}{o}", align_bytes=64)
-                w_bytes[i, o] = keep.tile([P, H], U8, name=f"w_bytes{i}{o}", align_bytes=64)
-        w3_raw = keep.tile([P, PACK, N], F32, name="w3_raw")
+                w_codes[i, o, 0] = keep.tile([P, H // 2], U32, name=f"w_codes{i}{o}", align_bytes=64)[:]
+                for pair in range(2):
+                    w_bytes[i, o, pair] = keep.tile([P, H // 2], U8, name=f"w_bytes{i}{o}{pair}", align_bytes=64)
         w3_bf = keep.tile([P, PACK * N], BF16, name="w3_bf", align_bytes=64)
         w3_codes = keep.tile([P, N], U32, name="w3_codes", align_bytes=64)
         w3_bytes = keep.tile([P, N], U8, name="w3_bytes", align_bytes=64)
         unit_t = keep.tile([P, PACK], F32, name="unit_t")
         own_gain = keep.tile([P, PACK], F32, name="own_gain")
         wave_gain = keep.tile([P, PACK], F32, name="wave_gain")
+        floor_at = keep.tile([P, 1], F32, name="floor_at")
         ln_floor = keep.tile([P, 1], F32, name="ln_floor")
         hid = keep.tile([P, PACK, S], BF16, name="hid")
 
+        identity = keep.tile([P, P], F32, name="identity")
+        make_identity(nc, identity[:])
         nc.vector.memset(xs_win[:].bitcast(I32), 0)
-        nc.vector.memset(ln_floor[:], LN_FLOOR)
+        nc.vector.memset(floor_at[:], FLOOR_AT)
+        nc.scalar.activation(ln_floor[:], floor_at[:], ACT.Sigmoid)
 
         def load_words(o):
             nc.sync.dma_start(out=x_win[o][:], in_=x_words[o].rearrange("p n t -> p (n t)").bitcast(I32))
@@ -78,56 +84,52 @@ def tile_picked_ygpusch_bal_p_kernel(
                 out=xs_win[32 * q : 32 * q + 4 * PASSES, :].bitcast(I32),
                 in_=x_scales[:, 4 * q : 4 * q + 4, :].bitcast(I32),
             )
+        nc.sync.dma_start(out=unit_t[:], in_=unit.rearrange("(p t) o -> p (t o)", t=PACK))
         load_weight(0, 0)
         load_words(1)
-        load_weight(1, 0)
         load_weight(0, 1)
+        load_weight(1, 0)
         load_weight(1, 1)
         nc.sync.dma_start(ovl_t[:], ovl)
-        nc.sync.dma_start(out=unit_t[:], in_=unit.rearrange("(p t) o -> p (t o)", t=PACK))
-        nc.sync.dma_start(out=w3_raw[:], in_=w3.rearrange("(p j) n -> p j n", j=PACK))
 
         def gather_words(o):
             nc.vector.tensor_copy(x_codes[o][:], x_win[o][:].bitcast(U32).indirect(offs_t[:]))
 
-        def round_weight(i, o, on_scalar):
+        def round_weight(i, o, scalar_share):
             whole_dst = w_bf[i, o][:].rearrange("p (t m j) -> p m j t", t=PACK, j=PACK)
             width = P // len(w_raw[i, o])
             for n, piece in enumerate(w_raw[i, o]):
                 dst = whole_dst[:, n * width : (n + 1) * width]
                 src = piece[:].rearrange("p j (m t) -> p m j t", t=PACK)
-                if on_scalar:
-                    nc.scalar.activation(dst, src, ACT.Copy)
-                else:
-                    nc.vector.tensor_copy(dst, src)
+                if scalar_share > 0:
+                    nc.scalar.activation(dst[:, :scalar_share], src[:, :scalar_share], ACT.Copy)
+                if scalar_share < width:
+                    nc.vector.tensor_copy(dst[:, scalar_share:], src[:, scalar_share:])
 
-        def quantize_weight(i, o, t0, t1):
-            cols = slice(t0 * P, t1 * P)
+        def quantize_weight(i, o, pair):
             nc.vector.quantize_mx(
-                out=w_codes[i, o][:, cols].bitcast(FP8X4),
-                scales=w_bytes[i, o][:, cols],
-                in_=w_bf[i, o][:, t0 * P * PACK : t1 * P * PACK],
+                out=w_codes[i, o, pair].bitcast(FP8X4),
+                scales=w_bytes[i, o, pair][:],
+                in_=w_bf[i, o][:, pair * 2 * H : (pair + 1) * 2 * H],
             )
 
         gather_words(0)
-        round_weight(0, 0, True)
+        round_weight(0, 0, P)
         nc.vector.tensor_copy(x_bytes[:], xs_win[:].indirect(offs_t[:]))
+        quantize_weight(0, 0, 0)
         gather_words(1)
-        round_weight(1, 0, True)
-        quantize_weight(0, 0, 0, 4)
-        quantize_weight(1, 0, 0, 4)
 
         banks = {}
 
         def product_pass(i, t, h, o):
             if o == 0:
                 banks[i, t, h] = psum.tile([P, BANK], F32, name=f"bank{i}{t}{h}", tag="bank")
-            m_cols = slice(t * P, (t + 1) * P)
+            pair, m_cols = t // 2, slice(t % 2 * P, (t % 2 + 1) * P)
             n_cols = slice(h * BANK, (h + 1) * BANK)
             nc.tensor.matmul_mx(
                 out=banks[i, t, h][:],
-                lhsT=w_codes[i, o][:, m_cols].bitcast(FP8X4),
-                lhsT_scale=w_bytes[i, o][:, m_cols],
+                lhsT=w_codes[i, o, pair][:, m_cols].bitcast(FP8X4),
+                lhsT_scale=w_bytes[i, o, pair][:, m_cols],
                 rhs=x_codes[o][:, n_cols].bitcast(FP8X4),
                 rhs_scale=x_bytes[4 * o : P, n_cols],
                 start=(o == 0),
@@ -161,58 +163,77 @@ def tile_picked_ygpusch_bal_p_kernel(
                 soft[i, t][:, cols], neg[t][:, i, cols], -1.0, banks[i, t, h][:], ALU.mult, ALU.max
             )
 
-        def look_up(t):
+        def look_up(t, scale):
             picked[t] = work.tile([P, S], F32, name=f"picked{t}", tag="picked")
             for h in range(HALVES):
                 nc.scalar.activation(
                     picked[t][:, h * BANK : (h + 1) * BANK],
                     soft[0, t][:].indirect(ovl_t[:, h * BANK // 16 : (h + 1) * BANK // 16]),
                     ACT.Copy,
+                    scale=scale,
                 )
 
-        def steps(t, cols, spare_scalar):
-            a, b = soft[0, t][:, cols], soft[1, t][:, cols]
+        def wave_steps(t, ex, cols):
             n = cols.stop - cols.start
-            roof = work.tile([P, n], F32, name=f"roof{t}", tag="roof")
-            part = work.tile([P, n], F32, name=f"part{t}", tag="part")
-            both = work.tile([P, n], F32, name=f"both{t}", tag="both")
-            hidd = work.tile([P, n], F32, name=f"hidd{t}", tag="hidd")
-            ex = work.tile([P, n], F32, name=f"ex{t}", tag="ex")
             wave = work.tile([P, n // 2], F32, name=f"wave{t}", tag="wave")
             wave_s = work.tile([P, n // 2], F32, name=f"wave_s{t}", tag="wave_s")
-            pairs = ex[:].rearrange("p (v d) -> p v d", d=2)
-
-            def scale_wave():
-                if spare_scalar:
-                    nc.scalar.activation(wave_s[:], wave[:], ACT.Copy, scale=wave_gain[:, t : t + 1])
-                else:
-                    nc.vector.tensor_scalar_mul(wave_s[:], wave[:], wave_gain[:, t : t + 1])
-
-            def make_hid(lo, hi):
-                nc.vector.scalar_tensor_tensor(
-                    hid[:, t, cols.start + lo : cols.start + hi].rearrange("p (v d) -> p v d", d=2),
-                    pairs[:, lo // 2 : hi // 2],
+            pairs = ex.rearrange("p (v d) -> p v d", d=2)
+            return [
+                lambda: nc.vector.tensor_tensor(wave[:], pairs[:, :, 0], pairs[:, :, 1], ALU.max),
+                lambda: nc.vector.tensor_scalar_mul(wave_s[:], wave[:], wave_gain[:, t : t + 1]),
+                lambda: nc.vector.scalar_tensor_tensor(
+                    hid[:, t, cols].rearrange("p (v d) -> p v d", d=2),
+                    pairs,
                     own_gain[:, t : t + 1],
-                    wave_s[:, lo // 2 : hi // 2].unsqueeze(2).to_broadcast([P, (hi - lo) // 2, 2]),
+                    wave_s[:].unsqueeze(2).to_broadcast([P, n // 2, 2]),
                     ALU.mult,
                     ALU.subtract,
-                )
+                ),
+            ]
 
-            return make_hid, [
+        def vector_steps(t):
+            a, b = soft[0, t][:], soft[1, t][:]
+            roof = work.tile([P, S], F32, name=f"roof{t}", tag="roof")
+            part = work.tile([P, S], F32, name=f"part{t}", tag="part")
+            both = work.tile([P, S], F32, name=f"both{t}", tag="both")
+            hidd = work.tile([P, S], F32, name=f"hidd{t}", tag="hidd")
+            ex = work.tile([P, S], F32, name=f"ex{t}", tag="ex")
+            return [
                 lambda: nc.vector.tensor_tensor(roof[:], a, b, ALU.max),
                 lambda: nc.vector.scalar_tensor_tensor(part[:], roof[:], 0.7 / 0.3, a, ALU.mult, ALU.add),
                 lambda: nc.vector.tensor_tensor(both[:], part[:], b, ALU.add),
-                lambda: nc.vector.tensor_tensor(hidd[:], picked[t][:, cols], b, ALU.min),
-                lambda: nc.vector.scalar_tensor_tensor(ex[:], hidd[:], -2.0, both[:], ALU.mult, ALU.add),
-                lambda: nc.vector.tensor_tensor(wave[:], pairs[:, :, 0], pairs[:, :, 1], ALU.max),
-                scale_wave,
-            ]
+                lambda: nc.vector.scalar_tensor_tensor(hidd[:], b, -2.0, picked[t][:], ALU.mult, ALU.max),
+                lambda: nc.vector.tensor_tensor(ex[:], hidd[:], both[:], ALU.add),
+            ] + wave_steps(t, ex[:], slice(0, S))
+
+        turned = {}
+
+        def add_turned(t, h, term, start, stop):
+            if start:
+                turned[t, h] = psum.tile([P, BANK], F32, name=f"turned{t}{h}", tag="bank")
+            for n in range(BANK // P):
+                nc.tensor.matmul(
+                    turned[t, h][:, n * P : (n + 1) * P],
+                    term[:, n * P : (n + 1) * P],
+                    identity[:],
+                    start=start and n == 0,
+                    stop=stop and n == BANK // P - 1,
+                    is_transpose=True,
+                )
+
+        def turn_back(t, h):
+            staged = work.tile([P, BANK], F32, name=f"staged{t}{h}", tag="staged", bufs=4)
+            nc.scalar.copy(staged[:], turned[t, h][:])
+            back = psum.tile([P, BANK], F32, name=f"back{t}{h}", tag="bank")
+            for n in range(BANK // P):
+                nc.tensor.transpose(back[:, n * P : (n + 1) * P], staged[:, n * P : (n + 1) * P], identity[:])
+            return back
 
         def finish(c, OUT_CHUNK, on_scalar):
             cols = slice(c, c + OUT_CHUNK)
-            grouped = work.tile([P, PACK * OUT_CHUNK], BF16, name=f"grouped{c}", tag="grouped", align_bytes=64)
-            h_codes = work.tile([P, OUT_CHUNK], U32, name=f"h_codes{c}", tag="h_codes", align_bytes=64)
-            h_bytes = work.tile([P, OUT_CHUNK], U8, name=f"h_bytes{c}", tag="h_bytes", align_bytes=64)
+            grouped = work.tile([P, PACK * OUT_CHUNK], BF16, name=f"grouped{c}", tag="grouped", bufs=4, align_bytes=64)
+            h_codes = work.tile([P, OUT_CHUNK], U32, name=f"h_codes{c}", tag="h_codes", bufs=4, align_bytes=64)
+            h_bytes = work.tile([P, OUT_CHUNK], U8, name=f"h_bytes{c}", tag="h_bytes", bufs=4, align_bytes=64)
             dst = grouped[:].rearrange("p (c i t) -> p c t i", i=4, t=PACK)
             src = hid[:, :, cols].rearrange("p t (c i) -> p c t i", i=4)
             if on_scalar:
@@ -230,24 +251,31 @@ def tile_picked_ygpusch_bal_p_kernel(
                 start=True,
                 stop=True,
             )
-            res = work.tile([P, OUT_CHUNK], F32, name=f"res{c}", tag="res")
-            nc.scalar.copy(res[:], acc[:, :OUT_CHUNK])
+            res = work.tile([P, OUT_CHUNK], F32, name=f"res{c}", tag="res", bufs=4)
+            if c + OUT_CHUNK < S:
+                nc.scalar.copy(res[:], acc[:, :OUT_CHUNK])
+            else:
+                nc.vector.tensor_copy(res[:], acc[:, :OUT_CHUNK])
             nc.sync.dma_start(out=out[:, cols], in_=res[:])
 
         first, second = (0, 1), (2, 3)
         for i in range(2):
-            for t in first:
-                for h in range(HALVES):
-                    product_pass(i, t, h, 0)
-        for i in range(2):
-            round_weight(i, 1, False)
-            quantize_weight(i, 1, 0, 2)
-            for t in first:
-                for h in range(HALVES):
-                    product_pass(i, t, h, 1)
+            for o in range(PASSES):
+                if (i, o) != (0, 0):
+                    round_weight(i, o, P // 2 if i == 0 else 0)
+                    quantize_weight(i, o, 0)
+                for t in first:
+                    for h in range(HALVES):
+                        product_pass(i, t, h, o)
         sigmoids(first)
+        w3_raw = keep.tile([P, PACK, N], F32, name="w3_raw", tag="w_raw100", align_bytes=64)
+        nc.sync.dma_start(out=w3_raw[:], in_=w3.rearrange("(p j) n -> p j n", j=PACK))
+        late_codes = keep.tile([P, 2 * PASSES * H // 2], U32, name="late_codes", tag="w_raw111", align_bytes=64)
         for i in range(2):
-            quantize_weight(i, 1, 2, 4)
+            for o in range(PASSES):
+                n = i * PASSES + o
+                w_codes[i, o, 1] = late_codes[:, n * H // 2 : (n + 1) * H // 2]
+                quantize_weight(i, o, 1)
         nc.vector.tensor_copy(
             w3_bf[:].rearrange("p (c i j) -> p c j i", i=4, j=PACK),
             w3_raw[:].rearrange("p j (c i) -> p c j i", i=4),
@@ -263,7 +291,7 @@ def tile_picked_ygpusch_bal_p_kernel(
                     for i in range(2):
                         softplus(i, t, h)
             for t in ts:
-                look_up(t)
+                look_up(t, -2.0)
 
         softplus_all(first)
         for i in range(2):
@@ -272,21 +300,34 @@ def tile_picked_ygpusch_bal_p_kernel(
                     for o in range(PASSES):
                         product_pass(i, t, h, o)
         sigmoids(second)
-        (hid0, steps0), (hid1, steps1) = steps(0, slice(0, S), False), steps(1, slice(0, S), False)
-        for one, other in zip(steps0, steps1):
+        for one, other in zip(vector_steps(0), vector_steps(1)):
             one()
             other()
-        hid0(0, S)
-        hid1(0, S)
         softplus_all(second)
-        for h in range(HALVES):
-            cols = slice(h * BANK, (h + 1) * BANK)
-            (hid2, steps2), (hid3, steps3) = steps(2, cols, True), steps(3, cols, True)
-            for one, other in zip(steps2, steps3):
+        halves = [slice(h * BANK, (h + 1) * BANK) for h in range(HALVES)]
+        for t in second:
+            for h, cols in enumerate(halves):
+                add_turned(t, h, soft[0, t][:, cols], True, False)
+                add_turned(t, h, soft[1, t][:, cols], False, False)
+        roof, back = {}, {}
+        for t in second:
+            hidd = work.tile([P, S], F32, name=f"hidd{t}", tag="hidd")
+            for h, cols in enumerate(halves):
+                nc.vector.scalar_tensor_tensor(
+                    hidd[:, cols], soft[1, t][:, cols], -2.0, picked[t][:, cols], ALU.mult, ALU.max
+                )
+                add_turned(t, h, hidd[:, cols], False, True)
+                back[t, h] = turn_back(t, h)
+            roof[t] = work.tile([P, S], F32, name=f"roof{t}", tag="roof")
+            nc.vector.tensor_tensor(roof[t][:], soft[0, t][:], soft[1, t][:], ALU.max)
+        ex = {t: work.tile([P, S], F32, name=f"ex{t}", tag="ex") for t in second}
+        for h, cols in enumerate(halves):
+            for t in second:
+                nc.vector.scalar_tensor_tensor(
+                    ex[t][:, cols], roof[t][:, cols], 0.7 / 0.3, back[t, h][:], ALU.mult, ALU.add
+                )
+            for one, other in zip(*[wave_steps(t, ex[t][:, cols], cols) for t in second]):
                 one()
                 other()
-            width = BANK if h < HALVES - 1 else BANK // 2
-            for lo in range(0, BANK, width):
-                hid2(lo, lo + width)
-                hid3(lo, lo + width)
-                finish(cols.start + lo, width, cols.start + lo + width < S)
+            for c in range(cols.start, cols.stop, BANK // 2):
+                finish(c, BANK // 2, c != BANK)

@@ -96,11 +96,11 @@ def tile_picked_ygpusch_bal_p_kernel(
             nc.vector.tensor_copy(x_codes[o][:], x_win[o][:].bitcast(U32).indirect(offs_t[:]))
 
         def round_weight(i, o, scalar_share):
-            whole_dst = w_bf[i, o][:].rearrange("p (t m j) -> p m j t", t=PACK, j=PACK)
+            whole_dst = w_bf[i, o][:].rearrange("p (t m j) -> p m t j", t=PACK, j=PACK)
             width = P // len(w_raw[i, o])
             for n, piece in enumerate(w_raw[i, o]):
                 dst = whole_dst[:, n * width : (n + 1) * width]
-                src = piece[:].rearrange("p j (m t) -> p m j t", t=PACK)
+                src = piece[:].rearrange("p j (m t) -> p m t j", t=PACK)
                 if scalar_share > 0:
                     nc.scalar.activation(dst[:, :scalar_share], src[:, :scalar_share], ACT.Copy)
                 if scalar_share < width:
@@ -164,7 +164,10 @@ def tile_picked_ygpusch_bal_p_kernel(
             )
 
         def look_up(t, scale):
-            picked[t] = work.tile([P, S], F32, name=f"picked{t}", tag="picked")
+            if t == 3:
+                picked[t] = work.tile([P, S], F32, name=f"picked{t}", tag="last_picked", bufs=1)
+            else:
+                picked[t] = work.tile([P, S], F32, name=f"picked{t}", tag="picked")
             for h in range(HALVES):
                 nc.scalar.activation(
                     picked[t][:, h * BANK : (h + 1) * BANK],
@@ -221,9 +224,8 @@ def tile_picked_ygpusch_bal_p_kernel(
                     is_transpose=True,
                 )
 
-        def turn_back(t, h):
-            staged = work.tile([P, BANK], F32, name=f"staged{t}{h}", tag="staged", bufs=4)
-            nc.scalar.copy(staged[:], turned[t, h][:])
+        def turn_back(t, h, staged):
+            nc.scalar.copy(staged, turned[t, h][:])
             back = psum.tile([P, BANK], F32, name=f"back{t}{h}", tag="bank")
             for n in range(BANK // P):
                 nc.tensor.transpose(back[:, n * P : (n + 1) * P], staged[:, n * P : (n + 1) * P], identity[:])
@@ -317,9 +319,12 @@ def tile_picked_ygpusch_bal_p_kernel(
                     hidd[:, cols], soft[1, t][:, cols], -2.0, picked[t][:, cols], ALU.mult, ALU.max
                 )
                 add_turned(t, h, hidd[:, cols], False, True)
-                back[t, h] = turn_back(t, h)
             roof[t] = work.tile([P, S], F32, name=f"roof{t}", tag="roof")
             nc.vector.tensor_tensor(roof[t][:], soft[0, t][:], soft[1, t][:], ALU.max)
+        staged = work.tile([P, HALVES, len(second), BANK], F32, name="staged", tag="last_picked", bufs=1)
+        for h in range(HALVES):
+            for n, t in enumerate(second):
+                back[t, h] = turn_back(t, h, staged[:, h, n])
         ex = {t: work.tile([P, S], F32, name=f"ex{t}", tag="ex") for t in second}
         for h, cols in enumerate(halves):
             for t in second:

@@ -96,11 +96,11 @@ def tile_picked_ygpusch_bal_p_kernel(
             nc.vector.tensor_copy(x_codes[o][:], x_win[o][:].bitcast(U32).indirect(offs_t[:]))
 
         def round_weight(i, o, scalar_share):
-            whole_dst = w_bf[i, o][:].rearrange("p (t m j) -> p m t j", t=PACK, j=PACK)
+            whole_dst = w_bf[i, o][:].rearrange("p (t m j) -> p m j t", t=PACK, j=PACK)
             width = P // len(w_raw[i, o])
             for n, piece in enumerate(w_raw[i, o]):
                 dst = whole_dst[:, n * width : (n + 1) * width]
-                src = piece[:].rearrange("p j (m t) -> p m t j", t=PACK)
+                src = piece[:].rearrange("p j (m t) -> p m j t", t=PACK)
                 if scalar_share > 0:
                     nc.scalar.activation(dst[:, :scalar_share], src[:, :scalar_share], ACT.Copy)
                 if scalar_share < width:
@@ -148,20 +148,22 @@ def tile_picked_ygpusch_bal_p_kernel(
                             sig[t][:, i, h * BANK : (h + 1) * BANK], banks[i, t, h][:], ACT.Sigmoid, scale=-1.0
                         )
 
+        def pieces_of(t):
+            edges = (0, BANK // 2, BANK, S) if t == 0 else (0, BANK, S)
+            return [slice(lo, hi) for lo, hi in zip(edges, edges[1:])]
+
         def logs(ts):
             for t in ts:
                 neg[t] = work.tile([P, 2, S], F32, name=f"neg{t}", tag="neg")
-                for h in range(HALVES):
-                    cols = slice(h * BANK, (h + 1) * BANK)
+                for cols in pieces_of(t):
                     nc.scalar.activation(neg[t][:, :, cols], sig[t][:, :, cols], ACT.Ln, bias=ln_floor[:])
 
-        def softplus(i, t, h):
-            if h == 0:
+        def softplus(i, t, cols):
+            if cols.start == 0:
                 soft[i, t] = keep.tile([P, S], F32, name=f"soft{i}{t}")
-            cols = slice(h * BANK, (h + 1) * BANK)
-            nc.vector.scalar_tensor_tensor(
-                soft[i, t][:, cols], neg[t][:, i, cols], -1.0, banks[i, t, h][:], ALU.mult, ALU.max
-            )
+            h = cols.start // BANK
+            sums = banks[i, t, h][:, cols.start - h * BANK : cols.stop - h * BANK]
+            nc.vector.scalar_tensor_tensor(soft[i, t][:, cols], neg[t][:, i, cols], -1.0, sums, ALU.mult, ALU.max)
 
         def look_up(t, scale):
             if t == 3:
@@ -289,9 +291,9 @@ def tile_picked_ygpusch_bal_p_kernel(
         def softplus_all(ts):
             logs(ts)
             for t in ts:
-                for h in range(HALVES):
+                for cols in pieces_of(t):
                     for i in range(2):
-                        softplus(i, t, h)
+                        softplus(i, t, cols)
             for t in ts:
                 look_up(t, -2.0)
 

from contextlib import ExitStack

import concourse.mybir as mybir
from concourse.masks import make_identity

K, T, S, H, N = 1024, 2048, 1024, 512, 128
FLOPS = 2 * (2 * K * H * S + H * N * S)

F32 = mybir.dt.float32
BF16 = mybir.dt.bfloat16
I32 = mybir.dt.int32
U32 = mybir.dt.uint32
U16 = mybir.dt.uint16
U8 = mybir.dt.uint8
FP8X4 = mybir.dt.float8_e4m3fn_x4
ALU = mybir.AluOpType
ACT = mybir.ActivationFunctionType

P = 128
PACK = 4
PASSES = K // (P * PACK)
BANK = 512
HALVES = S // BANK
FLOOR_AT = -40.0


def tile_picked_ygpusch_bal_p_kernel(
    tc, x_words, x_scales, w1, w2, unit, w3, offs, ovl, out
):
    nc = tc.nc
    with ExitStack() as ctx:
        keep = ctx.enter_context(tc.tile_pool(name="keep", bufs=1))
        work = ctx.enter_context(tc.tile_pool(name="work", bufs=2))
        psum = ctx.enter_context(tc.psum_pool(name="psum", bufs=8))

        offs_t = keep.tile([P, S // 16], U16, name="offs_t")
        ovl_t = keep.tile([P, S // 16], U16, name="ovl_t")
        x_win = [keep.tile([P, T], I32, name=f"x_win{o}", align_bytes=64) for o in range(PASSES)]
        xs_win = keep.tile([P, T], U8, name="xs_win", align_bytes=64)
        x_codes = [keep.tile([P, S], U32, name=f"x_codes{o}", align_bytes=64) for o in range(PASSES)]
        x_bytes = keep.tile([P, S], U8, name="x_bytes", align_bytes=64)
        weights = (w1, w2)
        w_raw, w_bf, w_codes, w_bytes = {}, {}, {}, {}
        for o in range(PASSES):
            for i in range(2):
                pieces = 2 if (i, o) == (1, PASSES - 1) else 1
                w_raw[i, o] = [
                    keep.tile([P, PACK, H // pieces], F32, name=f"w_raw{i}{o}{n}", tag=f"w_raw{i}{o}{n}", align_bytes=64)
                    for n in range(pieces)
                ]
                w_bf[i, o] = keep.tile([P, PACK * H], BF16, name=f"w_bf{i}{o}", align_bytes=64)
                w_codes[i, o, 0] = keep.tile([P, H // 2], U32, name=f"w_codes{i}{o}", align_bytes=64)[:]
                for pair in range(2):
                    w_bytes[i, o, pair] = keep.tile([P, H // 2], U8, name=f"w_bytes{i}{o}{pair}", align_bytes=64)
        w3_bf = keep.tile([P, PACK * N], BF16, name="w3_bf", align_bytes=64)
        w3_codes = keep.tile([P, N], U32, name="w3_codes", align_bytes=64)
        w3_bytes = keep.tile([P, N], U8, name="w3_bytes", align_bytes=64)
        unit_t = keep.tile([P, PACK], F32, name="unit_t")
        own_gain = keep.tile([P, PACK], F32, name="own_gain")
        wave_gain = keep.tile([P, PACK], F32, name="wave_gain")
        floor_at = keep.tile([P, 1], F32, name="floor_at")
        ln_floor = keep.tile([P, 1], F32, name="ln_floor")
        hid = keep.tile([P, PACK, S], BF16, name="hid")

        identity = keep.tile([P, P], F32, name="identity")
        make_identity(nc, identity[:])
        nc.vector.memset(xs_win[:].bitcast(I32), 0)
        nc.vector.memset(floor_at[:], FLOOR_AT)
        nc.scalar.activation(ln_floor[:], floor_at[:], ACT.Sigmoid)

        def load_words(o):
            nc.sync.dma_start(out=x_win[o][:], in_=x_words[o].rearrange("p n t -> p (n t)").bitcast(I32))

        def load_weight(i, o):
            rows = weights[i][o * P * PACK : (o + 1) * P * PACK, :].rearrange("(p j) c -> p j c", j=PACK)
            width = H // len(w_raw[i, o])
            for n, piece in enumerate(w_raw[i, o]):
                nc.sync.dma_start(out=piece[:], in_=rows[:, :, n * width : (n + 1) * width])

        nc.sync.dma_start(offs_t[:], offs)
        load_words(0)
        for q in range(4):
            nc.sync.dma_start(
                out=xs_win[32 * q : 32 * q + 4 * PASSES, :].bitcast(I32),
                in_=x_scales[:, 4 * q : 4 * q + 4, :].bitcast(I32),
            )
        nc.sync.dma_start(out=unit_t[:], in_=unit.rearrange("(p t) o -> p (t o)", t=PACK))
        load_weight(0, 0)
        load_words(1)
        load_weight(0, 1)
        load_weight(1, 0)
        load_weight(1, 1)
        nc.sync.dma_start(ovl_t[:], ovl)

        def gather_words(o):
            nc.vector.tensor_copy(x_codes[o][:], x_win[o][:].bitcast(U32).indirect(offs_t[:]))

        def round_weight(i, o, scalar_share):
            whole_dst = w_bf[i, o][:].rearrange("p (t m j) -> p m j t", t=PACK, j=PACK)
            width = P // len(w_raw[i, o])
            for n, piece in enumerate(w_raw[i, o]):
                dst = whole_dst[:, n * width : (n + 1) * width]
                src = piece[:].rearrange("p j (m t) -> p m j t", t=PACK)
                if scalar_share > 0:
                    nc.scalar.activation(dst[:, :scalar_share], src[:, :scalar_share], ACT.Copy)
                if scalar_share < width:
                    nc.vector.tensor_copy(dst[:, scalar_share:], src[:, scalar_share:])

        def quantize_weight(i, o, pair):
            nc.vector.quantize_mx(
                out=w_codes[i, o, pair].bitcast(FP8X4),
                scales=w_bytes[i, o, pair][:],
                in_=w_bf[i, o][:, pair * 2 * H : (pair + 1) * 2 * H],
            )

        gather_words(0)
        round_weight(0, 0, P)
        nc.vector.tensor_copy(x_bytes[:], xs_win[:].indirect(offs_t[:]))
        quantize_weight(0, 0, 0)
        gather_words(1)

        banks = {}

        def product_pass(i, t, h, o):
            if o == 0:
                banks[i, t, h] = psum.tile([P, BANK], F32, name=f"bank{i}{t}{h}", tag="bank")
            pair, m_cols = t // 2, slice(t % 2 * P, (t % 2 + 1) * P)
            n_cols = slice(h * BANK, (h + 1) * BANK)
            nc.tensor.matmul_mx(
                out=banks[i, t, h][:],
                lhsT=w_codes[i, o, pair][:, m_cols].bitcast(FP8X4),
                lhsT_scale=w_bytes[i, o, pair][:, m_cols],
                rhs=x_codes[o][:, n_cols].bitcast(FP8X4),
                rhs_scale=x_bytes[4 * o : P, n_cols],
                start=(o == 0),
                stop=(o == PASSES - 1),
            )

        sig, neg, soft, picked = {}, {}, {}, {}

        def sigmoids(ts):
            for t in ts:
                sig[t] = work.tile([P, 2, S], F32, name=f"sig{t}", tag="sig")
            for i in range(2):
                for t in ts:
                    for h in range(HALVES):
                        nc.scalar.activation(
                            sig[t][:, i, h * BANK : (h + 1) * BANK], banks[i, t, h][:], ACT.Sigmoid, scale=-1.0
                        )

        def pieces_of(t):
            edges = (0, BANK // 2, BANK, S) if t == 0 else (0, BANK, S)
            return [slice(lo, hi) for lo, hi in zip(edges, edges[1:])]

        def logs(ts):
            for t in ts:
                neg[t] = work.tile([P, 2, S], F32, name=f"neg{t}", tag="neg")
                for cols in pieces_of(t):
                    nc.scalar.activation(neg[t][:, :, cols], sig[t][:, :, cols], ACT.Ln, bias=ln_floor[:])

        def softplus(i, t, cols):
            if cols.start == 0:
                soft[i, t] = keep.tile([P, S], F32, name=f"soft{i}{t}")
            h = cols.start // BANK
            sums = banks[i, t, h][:, cols.start - h * BANK : cols.stop - h * BANK]
            nc.vector.scalar_tensor_tensor(soft[i, t][:, cols], neg[t][:, i, cols], -1.0, sums, ALU.mult, ALU.max)

        def look_up(t, scale):
            if t == 3:
                picked[t] = work.tile([P, S], F32, name=f"picked{t}", tag="last_picked", bufs=1)
            else:
                picked[t] = work.tile([P, S], F32, name=f"picked{t}", tag="picked")
            for h in range(HALVES):
                nc.scalar.activation(
                    picked[t][:, h * BANK : (h + 1) * BANK],
                    soft[0, t][:].indirect(ovl_t[:, h * BANK // 16 : (h + 1) * BANK // 16]),
                    ACT.Copy,
                    scale=scale,
                )

        def wave_steps(t, ex, cols):
            n = cols.stop - cols.start
            wave = work.tile([P, n // 2], F32, name=f"wave{t}", tag="wave")
            wave_s = work.tile([P, n // 2], F32, name=f"wave_s{t}", tag="wave_s")
            pairs = ex.rearrange("p (v d) -> p v d", d=2)
            return [
                lambda: nc.vector.tensor_tensor(wave[:], pairs[:, :, 0], pairs[:, :, 1], ALU.max),
                lambda: nc.vector.tensor_scalar_mul(wave_s[:], wave[:], wave_gain[:, t : t + 1]),
                lambda: nc.vector.scalar_tensor_tensor(
                    hid[:, t, cols].rearrange("p (v d) -> p v d", d=2),
                    pairs,
                    own_gain[:, t : t + 1],
                    wave_s[:].unsqueeze(2).to_broadcast([P, n // 2, 2]),
                    ALU.mult,
                    ALU.subtract,
                ),
            ]

        def vector_steps(t):
            a, b = soft[0, t][:], soft[1, t][:]
            roof = work.tile([P, S], F32, name=f"roof{t}", tag="roof")
            part = work.tile([P, S], F32, name=f"part{t}", tag="part")
            both = work.tile([P, S], F32, name=f"both{t}", tag="both")
            hidd = work.tile([P, S], F32, name=f"hidd{t}", tag="hidd")
            ex = work.tile([P, S], F32, name=f"ex{t}", tag="ex")
            return [
                lambda: nc.vector.tensor_tensor(roof[:], a, b, ALU.max),
                lambda: nc.vector.scalar_tensor_tensor(part[:], roof[:], 0.7 / 0.3, a, ALU.mult, ALU.add),
                lambda: nc.vector.tensor_tensor(both[:], part[:], b, ALU.add),
                lambda: nc.vector.scalar_tensor_tensor(hidd[:], b, -2.0, picked[t][:], ALU.mult, ALU.max),
                lambda: nc.vector.tensor_tensor(ex[:], hidd[:], both[:], ALU.add),
            ] + wave_steps(t, ex[:], slice(0, S))

        turned = {}

        def add_turned(t, h, term, start, stop):
            if start:
                turned[t, h] = psum.tile([P, BANK], F32, name=f"turned{t}{h}", tag="bank")
            for n in range(BANK // P):
                nc.tensor.matmul(
                    turned[t, h][:, n * P : (n + 1) * P],
                    term[:, n * P : (n + 1) * P],
                    identity[:],
                    start=start and n == 0,
                    stop=stop and n == BANK // P - 1,
                    is_transpose=True,
                )

        def turn_back(t, h, staged):
            nc.scalar.copy(staged, turned[t, h][:])
            back = psum.tile([P, BANK], F32, name=f"back{t}{h}", tag="bank")
            for n in range(BANK // P):
                nc.tensor.transpose(back[:, n * P : (n + 1) * P], staged[:, n * P : (n + 1) * P], identity[:])
            return back

        def finish(c, OUT_CHUNK, on_scalar):
            cols = slice(c, c + OUT_CHUNK)
            grouped = work.tile([P, PACK * OUT_CHUNK], BF16, name=f"grouped{c}", tag="grouped", bufs=4, align_bytes=64)
            h_codes = work.tile([P, OUT_CHUNK], U32, name=f"h_codes{c}", tag="h_codes", bufs=4, align_bytes=64)
            h_bytes = work.tile([P, OUT_CHUNK], U8, name=f"h_bytes{c}", tag="h_bytes", bufs=4, align_bytes=64)
            dst = grouped[:].rearrange("p (c i t) -> p c t i", i=4, t=PACK)
            src = hid[:, :, cols].rearrange("p t (c i) -> p c t i", i=4)
            if on_scalar:
                nc.scalar.copy(dst, src)
            else:
                nc.vector.tensor_copy(dst, src)
            nc.vector.quantize_mx(out=h_codes[:].bitcast(FP8X4), scales=h_bytes[:], in_=grouped[:])
            acc = psum.tile([P, BANK], F32, name=f"acc{c}", tag="bank")
            nc.tensor.matmul_mx(
                out=acc[:, :OUT_CHUNK],
                lhsT=w3_codes[:].bitcast(FP8X4),
                lhsT_scale=w3_bytes[:],
                rhs=h_codes[:].bitcast(FP8X4),
                rhs_scale=h_bytes[:],
                start=True,
                stop=True,
            )
            res = work.tile([P, OUT_CHUNK], F32, name=f"res{c}", tag="res", bufs=4)
            if c + OUT_CHUNK < S:
                nc.scalar.copy(res[:], acc[:, :OUT_CHUNK])
            else:
                nc.vector.tensor_copy(res[:], acc[:, :OUT_CHUNK])
            nc.sync.dma_start(out=out[:, cols], in_=res[:])

        first, second = (0, 1), (2, 3)
        for i in range(2):
            for o in range(PASSES):
                if (i, o) != (0, 0):
                    round_weight(i, o, P // 2 if i == 0 else 0)
                    quantize_weight(i, o, 0)
                for t in first:
                    for h in range(HALVES):
                        product_pass(i, t, h, o)
        sigmoids(first)
        w3_raw = keep.tile([P, PACK, N], F32, name="w3_raw", tag="w_raw100", align_bytes=64)
        nc.sync.dma_start(out=w3_raw[:], in_=w3.rearrange("(p j) n -> p j n", j=PACK))
        late_codes = keep.tile([P, 2 * PASSES * H // 2], U32, name="late_codes", tag="w_raw111", align_bytes=64)
        for i in range(2):
            for o in range(PASSES):
                n = i * PASSES + o
                w_codes[i, o, 1] = late_codes[:, n * H // 2 : (n + 1) * H // 2]
                quantize_weight(i, o, 1)
        nc.vector.tensor_copy(
            w3_bf[:].rearrange("p (c i j) -> p c j i", i=4, j=PACK),
            w3_raw[:].rearrange("p j (c i) -> p c j i", i=4),
        )
        nc.vector.tensor_scalar_mul(own_gain[:], unit_t[:], 1.5 * 0.3)
        nc.vector.tensor_scalar_mul(wave_gain[:], unit_t[:], 0.5 * 0.3)
        nc.vector.quantize_mx(out=w3_codes[:].bitcast(FP8X4), scales=w3_bytes[:], in_=w3_bf[:])

        def softplus_all(ts):
            logs(ts)
            for t in ts:
                for cols in pieces_of(t):
                    for i in range(2):
                        softplus(i, t, cols)
            for t in ts:
                look_up(t, -2.0)

        softplus_all(first)
        for i in range(2):
            for t in second:
                for h in range(HALVES):
                    for o in range(PASSES):
                        product_pass(i, t, h, o)
        sigmoids(second)
        for one, other in zip(vector_steps(0), vector_steps(1)):
            one()
            other()
        softplus_all(second)
        halves = [slice(h * BANK, (h + 1) * BANK) for h in range(HALVES)]
        for t in second:
            for h, cols in enumerate(halves):
                add_turned(t, h, soft[0, t][:, cols], True, False)
                add_turned(t, h, soft[1, t][:, cols], False, False)
        roof, back = {}, {}
        for t in second:
            hidd = work.tile([P, S], F32, name=f"hidd{t}", tag="hidd")
            for h, cols in enumerate(halves):
                nc.vector.scalar_tensor_tensor(
                    hidd[:, cols], soft[1, t][:, cols], -2.0, picked[t][:, cols], ALU.mult, ALU.max
                )
                add_turned(t, h, hidd[:, cols], False, True)
            roof[t] = work.tile([P, S], F32, name=f"roof{t}", tag="roof")
            nc.vector.tensor_tensor(roof[t][:], soft[0, t][:], soft[1, t][:], ALU.max)
        staged = work.tile([P, HALVES, len(second), BANK], F32, name="staged", tag="last_picked", bufs=1)
        for h in range(HALVES):
            for n, t in enumerate(second):
                back[t, h] = turn_back(t, h, staged[:, h, n])
        ex = {t: work.tile([P, S], F32, name=f"ex{t}", tag="ex") for t in second}
        for h, cols in enumerate(halves):
            for t in second:
                nc.vector.scalar_tensor_tensor(
                    ex[t][:, cols], roof[t][:, cols], 0.7 / 0.3, back[t, h][:], ALU.mult, ALU.add
                )
            for one, other in zip(*[wave_steps(t, ex[t][:, cols], cols) for t in second]):
                one()
                other()
            for c in range(cols.start, cols.stop, BANK // 2):
                finish(c, BANK // 2, c != BANK)
